import numpy as np
import ml_dtypes


def mxq(x, axis, fmt="e4m3"):
    dtype, down = {"e4m3": (ml_dtypes.float8_e4m3fn, 7), "e5m2": (ml_dtypes.float8_e5m2, 14)}[fmt]
    v = np.moveaxis(np.asarray(x, np.float32).astype(ml_dtypes.bfloat16).astype(np.float64), axis, -1)
    blocks = v.reshape(v.shape[:-1] + (-1, 32))
    amax = np.abs(blocks).max(-1, keepdims=True)
    byte = np.maximum(np.where(amax > 0, np.frexp(amax)[1] - 1 + 127, 0) - down, 1)
    scale = np.exp2(byte - 127.0)
    codes = (blocks / scale).astype(np.float32).astype(dtype).astype(np.float64)
    return np.moveaxis((codes * scale).reshape(v.shape), -1, axis)


WIDE = False


def mx_kscale(k):
    if not WIDE:
        return np.ones(k)
    levels = np.array([10, -10, 5, -5, 0])
    if k % 512:
        return np.exp2(np.random.permutation(np.resize(levels, k // 32))).repeat(32)
    a = np.empty((k // 512, 16))
    for p in range(k // 512):
        a[p, :8] = np.random.permutation(np.resize(levels, 8))
        for g in range(8):
            far = levels[np.abs(levels - a[p, g]) >= 10]
            a[p, g + 8] = far[np.random.randint(len(far))]
    return np.exp2(a.ravel()).repeat(32)


def f64(x):
    return np.asarray(x).astype(np.float64)


def striped(idx):
    return np.tile(np.asarray(idx).reshape(-1, 16).T, (8, 1)).astype(np.uint16)


def unstriped(offs):
    return offs[:16].T.reshape(-1).astype(np.int64)


E2M1 = np.array([0.0, 0.5, 1.0, 1.5, 2.0, 3.0, 4.0, 6.0, -0.0, -0.5, -1.0, -1.5, -2.0, -3.0, -4.0, -6.0])


def pack_weight(w, fmt):
    k, n = w.shape
    w = f64(np.asarray(w, np.float32).astype(ml_dtypes.bfloat16)).reshape(k // 32, 32, n)
    amax = np.abs(w).max(1)
    if fmt == "e4m3":
        byte = np.frexp(amax)[1] - 1 + 127 - 7
    else:
        mant, ex = np.frexp(amax / 6.0)
        byte = np.where(mant > 0.5, ex, ex - 1) + 127
    byte = np.clip(np.where(amax > 0, byte, 1), 1, 254)
    scaled = (w * np.exp2(127.0 - byte)[:, None, :]).reshape(k, n).astype(np.float32)
    by_word = np.ascontiguousarray(scaled.reshape(k // 512, 128, 4, n).transpose(0, 1, 3, 2))
    if fmt == "e4m3":
        words = by_word.astype(ml_dtypes.float8_e4m3fn).view(np.uint8)
    else:
        c = by_word.astype(ml_dtypes.float4_e2m1fn).view(np.uint8) & 0xF
        words = (c[..., 0::2] | (c[..., 1::2] << 4)).reshape(k // 512, 128, 2 * n)
    return np.ascontiguousarray(words), np.ascontiguousarray(byte.astype(np.uint8).reshape(k // 512, 16, n))


def unpack_weight(words, scales, fmt):
    g, _, n = scales.shape
    words = np.ascontiguousarray(words).reshape(g, 128, n, -1)
    if fmt == "e4m3":
        vals = words.view(ml_dtypes.float8_e4m3fn).astype(np.float64)
    else:
        nib = np.empty((g, 128, n, 4), np.uint8)
        nib[..., 0::2] = words & 0xF
        nib[..., 1::2] = words >> 4
        vals = E2M1[nib]
    vals = vals * np.repeat(np.exp2(scales.astype(np.float64) - 127.0), 8, axis=1)[..., None]
    return vals.transpose(0, 1, 3, 2).reshape(g * 512, n)


def softplus(v):
    return np.log(1.0 + np.exp(v))


def sigmoid(v):
    return 1.0 / (1.0 + np.exp(-v))


D, T, U, I, J, G = 512, 1024, 1024, 256, 512, 128


def setup_inputs():
    n = np.random.standard_normal
    idx = np.random.permutation(T)[:I]
    idx2 = np.random.permutation(U)[:J]
    fd = mx_kscale(D)
    fj = mx_kscale(J)
    tj = np.ones(U)
    tj[idx2] = fj
    tabbp = pack_weight(n((D, U)) / fd[:, None], "e2m1")
    return {
        "taba": (n((D, T)) * 1 / np.sqrt(D) * fd[:, None]).astype(np.float32),
        "tabb_words": tabbp[0],
        "tabb_scales": tabbp[1],
        "stake": (n((I, G)) * 4.0).astype(np.float32),
        "bias": (np.random.uniform(0.0, 2.0, (1, J))).astype(np.float32),
        "js": (np.random.uniform(0.5, 2.0, (1, J)) * fj).astype(np.float32),
        "brows": (n((D, U)) / tj).astype(np.float32),
        "old": (n((D, T)) * 2.0).astype(np.float32),
        "fade": (np.random.uniform(0.5, 1.0, (1, T))).astype(np.float32),
        "offs": striped(idx),
        "offs2": striped(idx2),
    }


def reference(taba, tabb_words, tabb_scales, stake, bias, js, brows, old, fade, offs, offs2):
    idx = unstriped(offs)
    idx2 = unstriped(offs2)
    tabbu = unpack_weight(tabb_words, tabb_scales, "e2m1")
    tabaidxq = mxq(f64(taba)[:, idx], 0, "e4m3")
    tabbidx2g = tabbu[:, idx2]
    s = tabaidxq.T @ tabbidx2g
    u1 = softplus((s + f64(bias)) * (-1.0))
    ch = np.exp(u1.reshape(I, G, J // G).sum(axis=2) * (-1.0))
    dch = f64(stake) / (ch + 1.0)
    e1 = dch * ch * (-1.0)
    r1 = np.repeat(e1, J // G, axis=1)
    ds = r1 * sigmoid((s + f64(bias)) * (-1.0)) * (-1.0)
    gs = ds * f64(js)
    gt1 = gs.T
    bt = f64(brows)[:, idx2].T
    btq = mxq(bt, 0, "e4m3")
    gt1q = mxq(gt1, 0, "e4m3")
    gx1 = btq.T @ gt1q
    gf = np.zeros((D, T))
    gf[:, idx] = gx1
    y = f64(old) * f64(fade) + gf
    return y

@@ -1,0 +1,245 @@
+from contextlib import ExitStack
+
+import concourse.mybir as mybir
+from concourse.masks import make_identity
+
+D, T, U, I, J, G = 512, 1024, 1024, 256, 512, 128
+FLOPS = 2 * D * I * J + 2 * J * D * I
+
+F32 = mybir.dt.float32
+BF16 = mybir.dt.bfloat16
+I32 = mybir.dt.int32
+U32 = mybir.dt.uint32
+U16 = mybir.dt.uint16
+U8 = mybir.dt.uint8
+FP8X4 = mybir.dt.float8_e4m3fn_x4
+FP4X4 = mybir.dt.float4_e2m1fn_x4
+ACT = mybir.ActivationFunctionType
+ALU = mybir.AluOpType
+
+P = 128
+PACK = 4
+BANK = 512
+BLOCKS = D // P
+VECTOR_BLOCKS = (1, 2)
+
+
+def tile_attend_bpairteams_x_kernel(tc, taba, tabb_words, tabb_scales, stake, bias, js, brows, old, fade, offs, offs2, out):
+    nc = tc.nc
+    with ExitStack() as ctx:
+        lists = ctx.enter_context(tc.tile_pool(name="lists", bufs=1))
+        sb = ctx.enter_context(tc.tile_pool(name="sb", bufs=1))
+        psum = ctx.enter_context(tc.psum_pool(name="psum", bufs=1))
+
+        scale_pool = sb.tile([P, U], U8, name="scale_pool")
+        nc.vector.memset(scale_pool[:].bitcast(I32), 0)
+        list_j = lists.tile([P, J // 16], U16, name="list_j")
+        nc.sync.dma_start(list_j[:], offs2)
+        word_pool = sb.tile([P, U], U16, name="word_pool")
+        nc.sync.dma_start(word_pool[:].bitcast(I32), tabb_words[0].bitcast(I32))
+        b_blocks = [sb.tile([P, U], F32, name="b_block%d" % b) for b in range(BLOCKS)]
+        nc.sync.dma_start(b_blocks[0][:], brows[0:P, :])
+        taba_rows = taba.rearrange("(p t) u -> p t u", t=PACK)
+        a01 = sb.tile([P, 2, T], F32, name="a01")
+        nc.sync.dma_start(a01[:], taba_rows[:, 0:2, :])
+        list_i = lists.tile([P, I // 16], U16, name="list_i")
+        nc.sync.dma_start(list_i[:], offs)
+        for q in range(4):
+            nc.scalar.dma_start(
+                scale_pool[32 * q : 32 * q + 4, :].bitcast(I32), tabb_scales[0, 4 * q : 4 * q + 4, :].bitcast(I32)
+            )
+        a_planes = [a01[:, 0, :], a01[:, 1, :]]
+        for t in (2, 3):
+            plane = sb.tile([P, T], F32, name="a_plane%d" % t)
+            nc.sync.dma_start(plane[:], taba_rows[:, t, :])
+            a_planes.append(plane[:])
+        bias_col = sb.tile([P, PACK], F32, name="bias_col")
+        nc.scalar.dma_start(bias_col[:], bias[0].rearrange("(p r) -> p r", r=PACK))
+        js_col = sb.tile([P, PACK], F32, name="js_col")
+        nc.scalar.dma_start(js_col[:], js[0].rearrange("(p r) -> p r", r=PACK))
+        stake_rows = sb.tile([P, I // P, G], F32, name="stake_rows")
+        for b in range(1, BLOCKS):
+            nc.sync.dma_start(b_blocks[b][:], brows[P * b : P * (b + 1), :])
+            if b == 1:
+                nc.sync.dma_start(stake_rows[:], stake.rearrange("(h p) g -> p h g", p=P))
+        fade_rows = sb.tile([P, P], F32, name="fade_rows")
+        nc.gpsimd.memset(fade_rows[:], 0.0)
+        nc.gpsimd.dma_start(fade_rows[0 : T // P, :], fade[0].rearrange("(c p) -> c p", p=P))
+        old_halves = []
+        for h in range(T // BANK):
+            half = sb.tile([P, BLOCKS, BANK], F32, name="old_half%d" % h)
+            nc.sync.dma_start(half[:], old[:, BANK * h : BANK * (h + 1)].rearrange("(b p) t -> p b t", p=P))
+            old_halves.append(half)
+
+        ident = sb.tile([P, P], F32, name="ident")
+        make_identity(nc, ident[:])
+        warm = sb.tile([P, 1], F32, name="warm")
+        nc.scalar.activation(warm[:], ident[:, 0:1], ACT.Sigmoid)
+
+        windows = []
+        for b in range(BLOCKS):
+            window = sb.tile([P, T], F32, name="window%d" % b)
+            nc.vector.memset(window[:], 0.0)
+            windows.append(window)
+
+        def gather_brows(b):
+            columns = sb.tile([P, J], BF16, name="b_picked%d" % b)
+            if b in VECTOR_BLOCKS:
+                nc.vector.tensor_copy(columns[:], b_blocks[b][:].indirect(list_j[:]))
+            else:
+                narrow = sb.tile([P, U], BF16, name="b_narrow%d" % b)
+                nc.scalar.activation(narrow[:], b_blocks[b][:], ACT.Copy)
+                nc.scalar.activation(columns[:], narrow[:].indirect(list_j[:]), ACT.Copy)
+            return columns
+
+        picked = [gather_brows(0)]
+
+        words_j = sb.tile([P, J], U16, name="words_j")
+        nc.vector.tensor_copy(words_j[:], word_pool[:].indirect(list_j[:]))
+        words_dealt = sb.tile([P, PACK, G], U16, name="words_dealt", align_bytes=64)
+        nc.vector.tensor_copy(words_dealt[:], words_j[:].rearrange("p (g r) -> p r g", r=PACK))
+        scales_j = sb.tile([P, J], U8, name="scales_j")
+        nc.vector.tensor_copy(scales_j[:], scale_pool[:].indirect(list_j[:]))
+        scales_dealt = sb.tile([P, PACK, G], U8, name="scales_dealt", align_bytes=64)
+        nc.vector.tensor_copy(scales_dealt[:], scales_j[:].rearrange("p (g r) -> p r g", r=PACK))
+
+        a_woven = sb.tile([P, I, PACK], BF16, name="a_woven", align_bytes=64)
+        for t in range(PACK):
+            nc.vector.tensor_copy(a_woven[:, :, t], a_planes[t].indirect(list_i[:]))
+        a_codes = sb.tile([P, I], U32, name="a_codes", align_bytes=64)
+        a_scales = sb.tile([P, I], U8, name="a_scales", align_bytes=64)
+        nc.vector.quantize_mx(
+            out=a_codes[:].bitcast(FP8X4), scales=a_scales[:], in_=a_woven[:].rearrange("p i t -> p (i t)")
+        )
+        neg_bias = sb.tile([P, PACK], F32, name="neg_bias")
+        nc.gpsimd.tensor_scalar(neg_bias[:], bias_col[:], -1.0, 0.0, ALU.mult, ALU.add)
+
+        scores = []
+        for pair in range(2):
+            bank = psum.tile([P, 2, I], F32, name="scores%d" % pair, tag="mx", bufs=2)
+            for e in range(2):
+                r = 2 * pair + e
+                nc.tensor.matmul_mx(
+                    out=bank[:, e, :],
+                    lhsT=words_dealt[:, r, :].bitcast(FP4X4),
+                    lhsT_scale=scales_dealt[:, r, :],
+                    rhs=a_codes[:].bitcast(FP8X4),
+                    rhs_scale=a_scales[:],
+                    start=True,
+                    stop=True,
+                )
+                scores.append(bank[:, e, :])
+
+        small = psum.tile([P, I + P], F32, name="small")
+        for h in range(I // P):
+            nc.tensor.transpose(small[:, P * h : P * (h + 1)], stake_rows[:, h, :], ident[:])
+        nc.tensor.transpose(small[:, I : I + P], fade_rows[:], ident[:])
+
+        b_woven = [sb.tile([P, 2 * P, PACK], BF16, name="b_woven%d" % pair, align_bytes=64) for pair in range(2)]
+        b_codes = [sb.tile([P, 2 * P], U32, name="b_codes%d" % pair, align_bytes=64) for pair in range(2)]
+        b_scales = [sb.tile([P, 2 * P], U8, name="b_scales%d" % pair, align_bytes=64) for pair in range(2)]
+
+        def turn_brows(pair, two):
+            bank = psum.tile([P, 2, 2, P], F32, name="b_turned%d" % pair, tag="turn", bufs=2)
+            for e in range(2):
+                pairs = two[e][:].bitcast(F32)
+                for u in range(2):
+                    nc.tensor.transpose(bank[:, e, u, :], pairs[:, u : J // 2 : 2], ident[:])
+            nc.scalar.copy(
+                b_woven[pair][:].rearrange("p d t -> p (d t)").bitcast(F32).rearrange("p (e d u) -> p e d u", e=2, u=2),
+                bank[:].rearrange("p e u d -> p e d u"),
+            )
+
+        def quantise_brows(pair):
+            nc.vector.quantize_mx(
+                out=b_codes[pair][:].bitcast(FP8X4),
+                scales=b_scales[pair][:],
+                in_=b_woven[pair][:].rearrange("p d t -> p (d t)"),
+            )
+
+        picked.append(gather_brows(1))
+        picked.append(gather_brows(2))
+
+        pos = sb.tile([P, PACK, I], F32, name="pos")
+        neg = sb.tile([P, PACK, I], F32, name="neg")
+        neg_js = sb.tile([P, PACK, I], F32, name="neg_js")
+        for r in range(PACK):
+            nc.scalar.activation(pos[:, r, :], scores[r], ACT.Sigmoid, bias=bias_col[:, r : r + 1])
+        for r in range(PACK):
+            nc.scalar.activation(neg[:, r, :], scores[r], ACT.Sigmoid, bias=neg_bias[:, r : r + 1], scale=-1.0)
+        for r in range(PACK):
+            nc.scalar.activation(neg_js[:, r, :], neg[:, r, :], ACT.Copy, scale=js_col[:, r : r + 1])
+        turn_brows(0, picked[0:2])
+        picked.append(gather_brows(3))
+        turn_brows(1, picked[2:4])
+        low = sb.tile([P, I], F32, name="low")
+        high = sb.tile([P, I], F32, name="high")
+        chance = sb.tile([P, I], F32, name="chance")
+        nc.vector.tensor_tensor(low[:], pos[:, 0, :], pos[:, 1, :], ALU.mult)
+        nc.vector.tensor_tensor(high[:], pos[:, 2, :], pos[:, 3, :], ALU.mult)
+        nc.vector.tensor_tensor(chance[:], low[:], high[:], ALU.mult)
+        plus_one = sb.tile([P, I], F32, name="plus_one")
+        nc.vector.tensor_scalar_add(plus_one[:], chance[:], 1.0)
+        staked = sb.tile([P, I], F32, name="staked")
+        nc.vector.tensor_tensor(staked[:], small[:, 0:I], chance[:], ALU.mult)
+        inverse = sb.tile([P, I], F32, name="inverse")
+        nc.vector.reciprocal(inverse[:], plus_one[:])
+        team = sb.tile([P, I], F32, name="team")
+        nc.vector.tensor_tensor(team[:], staked[:], inverse[:], ALU.mult)
+        quantise_brows(0)
+        g_woven = sb.tile([P, I, PACK], BF16, name="g_woven", align_bytes=64)
+        nc.vector.tensor_tensor(
+            g_woven[:].rearrange("p (c i) r -> p c r i", i=4),
+            neg_js[:].rearrange("p r (c i) -> p c r i", i=4),
+            team[:].rearrange("p (c i) -> p c i", i=4).unsqueeze(2).to_broadcast([P, I // 4, PACK, 4]),
+            ALU.mult,
+        )
+        g_codes = sb.tile([P, I], U32, name="g_codes", align_bytes=64)
+        g_scales = sb.tile([P, I], U8, name="g_scales", align_bytes=64)
+        nc.vector.quantize_mx(
+            out=g_codes[:].bitcast(FP8X4), scales=g_scales[:], in_=g_woven[:].rearrange("p i r -> p (i r)")
+        )
+        fade_col = sb.tile([P, T // P], F32, name="fade_col")
+        nc.scalar.copy(fade_col[:], small[:, I : I + T // P])
+
+        def second_product(pair):
+            bank = psum.tile([P, 2, I], F32, name="grad%d" % pair, tag="mx", bufs=2)
+            for e in range(2):
+                nc.tensor.matmul_mx(
+                    out=bank[:, e, :],
+                    lhsT=b_codes[pair][:, P * e : P * (e + 1)].bitcast(FP8X4),
+                    lhsT_scale=b_scales[pair][:, P * e : P * (e + 1)],
+                    rhs=g_codes[:].bitcast(FP8X4),
+                    rhs_scale=g_scales[:],
+                    start=True,
+                    stop=True,
+                )
+            for e in range(2):
+                grad = sb.tile([P, I], F32, name="grad_sb%d" % (2 * pair + e))
+                nc.scalar.copy(grad[:], bank[:, e, :])
+                nc.vector.tensor_copy(windows[2 * pair + e][:].indirect(list_i[:]), grad[:])
+
+        quantise_brows(1)
+        second_product(0)
+        second_product(1)
+
+        faded = []
+        for c in range(T // P):
+            bank = psum.tile([P, 2, 2, P], F32, name="old_turned%d" % c, tag="turn", bufs=2)
+            flat = bank[:].rearrange("p e u d -> p (e u d)")
+            h, col = divmod(P * c, BANK)
+            for b in range(BLOCKS):
+                nc.tensor.transpose(flat[:, P * b : P * (b + 1)], old_halves[h][:, b, col : col + P], ident[:])
+            chunk = sb.tile([P, D], F32, name="faded%d" % c)
+            nc.scalar.activation(chunk[:], flat, ACT.Copy, scale=fade_col[:, c : c + 1])
+            faded.append(chunk)
+
+        for b in range(BLOCKS):
+            for h in range(T // BANK):
+                bank = psum.tile([P, BANK], F32, name="back%d_%d" % (b, h), tag="back", bufs=3)
+                for k in range(BANK // P):
+                    c = h * (BANK // P) + k
+                    nc.tensor.transpose(bank[:, P * k : P * (k + 1)], faded[c][:, P * b : P * (b + 1)], ident[:])
+                result = sb.tile([P, BANK], F32, name="result%d_%d" % (b, h))
+                nc.vector.tensor_tensor(result[:], bank[:], windows[b][:, BANK * h : BANK * (h + 1)], ALU.add)
+                nc.sync.dma_start(out[P * b : P * (b + 1), BANK * h : BANK * (h + 1)], result[:])

@@ -22,6 +22,8 @@ PACK = 4
 BANK = 512
 BLOCKS = D // P
 VECTOR_BLOCKS = (1, 2)
+WINDOWS = 3
+POOL_BLOCKS = 2
 
 
 def tile_attend_bpairteams_x_kernel(tc, taba, tabb_words, tabb_scales, stake, bias, js, brows, old, fade, offs, offs2, out):
@@ -65,11 +67,11 @@ def tile_attend_bpairteams_x_kernel(tc, taba, tabb_words, tabb_scales, stake, bi
         fade_rows = sb.tile([P, P], F32, name="fade_rows")
         nc.gpsimd.memset(fade_rows[:], 0.0)
         nc.gpsimd.dma_start(fade_rows[0 : T // P, :], fade[0].rearrange("(c p) -> c p", p=P))
-        old_halves = []
-        for h in range(T // BANK):
-            half = sb.tile([P, BLOCKS, BANK], F32, name="old_half%d" % h)
-            nc.sync.dma_start(half[:], old[:, BANK * h : BANK * (h + 1)].rearrange("(b p) t -> p b t", p=P))
-            old_halves.append(half)
+        old_blocks = []
+        for b in range(BLOCKS):
+            block = sb.tile([P, T], F32, name="old_block%d" % b)
+            nc.sync.dma_start(block[:], old[P * b : P * (b + 1), :])
+            old_blocks.append(block)
 
         ident = sb.tile([P, P], F32, name="ident")
         make_identity(nc, ident[:])
@@ -77,7 +79,7 @@ def tile_attend_bpairteams_x_kernel(tc, taba, tabb_words, tabb_scales, stake, bi
         nc.scalar.activation(warm[:], ident[:, 0:1], ACT.Sigmoid)
 
         windows = []
-        for b in range(BLOCKS):
+        for b in range(WINDOWS):
             window = sb.tile([P, T], F32, name="window%d" % b)
             nc.vector.memset(window[:], 0.0)
             windows.append(window)
@@ -93,6 +95,18 @@ def tile_attend_bpairteams_x_kernel(tc, taba, tabb_words, tabb_scales, stake, bi
             return columns
 
         picked = [gather_brows(0)]
+
+        fade_turned = psum.tile([P, BANK], F32, name="fade_turned", tag="back", bufs=3)
+        nc.tensor.transpose(fade_turned[:, 0:P], fade_rows[:], ident[:])
+        fade_col = sb.tile([P, T // P], F32, name="fade_col")
+        nc.scalar.copy(fade_col[:], fade_turned[:, 0 : T // P])
+        fade_all = sb.tile([P, T], F32, name="fade_all")
+        for h in range(T // BANK):
+            bank = psum.tile([P, BANK], F32, name="fade_spread%d" % h, tag="back", bufs=3)
+            for k in range(BANK // P):
+                c = h * (BANK // P) + k
+                nc.tensor.transpose(bank[:, P * k : P * (k + 1)], fade_col[:, c : c + 1].to_broadcast([P, P]), ident[:])
+            nc.scalar.copy(fade_all[:, BANK * h : BANK * (h + 1)], bank[:])
 
         words_j = sb.tile([P, J], U16, name="words_j")
         nc.vector.tensor_copy(words_j[:], word_pool[:].indirect(list_j[:]))
@@ -130,10 +144,9 @@ def tile_attend_bpairteams_x_kernel(tc, taba, tabb_words, tabb_scales, stake, bi
                 )
                 scores.append(bank[:, e, :])
 
-        small = psum.tile([P, I + P], F32, name="small")
+        small = psum.tile([P, I], F32, name="small")
         for h in range(I // P):
             nc.tensor.transpose(small[:, P * h : P * (h + 1)], stake_rows[:, h, :], ident[:])
-        nc.tensor.transpose(small[:, I : I + P], fade_rows[:], ident[:])
 
         b_woven = [sb.tile([P, 2 * P, PACK], BF16, name="b_woven%d" % pair, align_bytes=64) for pair in range(2)]
         b_codes = [sb.tile([P, 2 * P], U32, name="b_codes%d" % pair, align_bytes=64) for pair in range(2)]
@@ -174,7 +187,7 @@ def tile_attend_bpairteams_x_kernel(tc, taba, tabb_words, tabb_scales, stake, bi
         turn_brows(1, picked[2:4])
         low = sb.tile([P, I], F32, name="low")
         high = sb.tile([P, I], F32, name="high")
-        chance = sb.tile([P, I], F32, name="chance")
+        chance = sb.tile([P, I], F32, name="chance", tag="hold0", align_bytes=64)
         nc.vector.tensor_tensor(low[:], pos[:, 0, :], pos[:, 1, :], ALU.mult)
         nc.vector.tensor_tensor(high[:], pos[:, 2, :], pos[:, 3, :], ALU.mult)
         nc.vector.tensor_tensor(chance[:], low[:], high[:], ALU.mult)
@@ -187,59 +200,82 @@ def tile_attend_bpairteams_x_kernel(tc, taba, tabb_words, tabb_scales, stake, bi
         team = sb.tile([P, I], F32, name="team")
         nc.vector.tensor_tensor(team[:], staked[:], inverse[:], ALU.mult)
         quantise_brows(0)
-        g_woven = sb.tile([P, I, PACK], BF16, name="g_woven", align_bytes=64)
-        nc.vector.tensor_tensor(
-            g_woven[:].rearrange("p (c i) r -> p c r i", i=4),
-            neg_js[:].rearrange("p r (c i) -> p c r i", i=4),
-            team[:].rearrange("p (c i) -> p c i", i=4).unsqueeze(2).to_broadcast([P, I // 4, PACK, 4]),
-            ALU.mult,
-        )
         g_codes = sb.tile([P, I], U32, name="g_codes", align_bytes=64)
         g_scales = sb.tile([P, I], U8, name="g_scales", align_bytes=64)
-        nc.vector.quantize_mx(
-            out=g_codes[:].bitcast(FP8X4), scales=g_scales[:], in_=g_woven[:].rearrange("p i r -> p (i r)")
-        )
-        fade_col = sb.tile([P, T // P], F32, name="fade_col")
-        nc.scalar.copy(fade_col[:], small[:, I : I + T // P])
+        grads = [sb.tile([P, 2, I], F32, name="grads%d" % pair) for pair in range(2)]
 
-        def second_product(pair):
-            bank = psum.tile([P, 2, I], F32, name="grad%d" % pair, tag="mx", bufs=2)
+        def second_product(pair, bank, cols):
             for e in range(2):
                 nc.tensor.matmul_mx(
                     out=bank[:, e, :],
                     lhsT=b_codes[pair][:, P * e : P * (e + 1)].bitcast(FP8X4),
                     lhsT_scale=b_scales[pair][:, P * e : P * (e + 1)],
-                    rhs=g_codes[:].bitcast(FP8X4),
-                    rhs_scale=g_scales[:],
+                    rhs=g_codes[:, cols].bitcast(FP8X4),
+                    rhs_scale=g_scales[:, cols],
                     start=True,
                     stop=True,
                 )
-            for e in range(2):
-                grad = sb.tile([P, I], F32, name="grad_sb%d" % (2 * pair + e))
-                nc.scalar.copy(grad[:], bank[:, e, :])
-                nc.vector.tensor_copy(windows[2 * pair + e][:].indirect(list_i[:]), grad[:])
 
-        quantise_brows(1)
-        second_product(0)
-        second_product(1)
+        first_bank = psum.tile([P, 2, 2, P], F32, name="grad_first", tag="mx", bufs=2)
+        for h in range(I // P):
+            cols = slice(P * h, P * (h + 1))
+            g_woven = sb.tile([P, P, PACK], BF16, name="g_woven%d" % h, tag="hold1", align_bytes=64)
+            nc.vector.tensor_tensor(
+                g_woven[:].rearrange("p (c i) r -> p c r i", i=4),
+                neg_js[:, :, cols].rearrange("p r (c i) -> p c r i", i=4),
+                team[:, cols].rearrange("p (c i) -> p c i", i=4).unsqueeze(2).to_broadcast([P, P // 4, PACK, 4]),
+                ALU.mult,
+            )
+            if h == 0:
+                quantise_brows(1)
+            nc.vector.quantize_mx(
+                out=g_codes[:, cols].bitcast(FP8X4), scales=g_scales[:, cols], in_=g_woven[:].rearrange("p i r -> p (i r)")
+            )
+            second_product(0, first_bank[:, h, :, :], cols)
+            nc.scalar.copy(grads[0][:, :, cols], first_bank[:, h, :, :])
+        second_bank = psum.tile([P, 2, I], F32, name="grad_second", tag="mx", bufs=2)
+        second_product(1, second_bank[:], slice(0, I))
+        nc.scalar.copy(grads[1][:], second_bank[:])
 
+        kept = []
+        for b in range(POOL_BLOCKS):
+            product = sb.tile([P, T], F32, name="kept%d" % b, tag="hold%d" % b, align_bytes=64)
+            nc.gpsimd.tensor_tensor(product[:], old_blocks[b][:], fade_all[:], ALU.mult)
+            kept.append(product)
+
+        turned_blocks = BLOCKS - POOL_BLOCKS
+        per_bank = BANK // (P * turned_blocks)
         faded = []
-        for c in range(T // P):
-            bank = psum.tile([P, 2, 2, P], F32, name="old_turned%d" % c, tag="turn", bufs=2)
-            flat = bank[:].rearrange("p e u d -> p (e u d)")
-            h, col = divmod(P * c, BANK)
-            for b in range(BLOCKS):
-                nc.tensor.transpose(flat[:, P * b : P * (b + 1)], old_halves[h][:, b, col : col + P], ident[:])
-            chunk = sb.tile([P, D], F32, name="faded%d" % c)
-            nc.scalar.activation(chunk[:], flat, ACT.Copy, scale=fade_col[:, c : c + 1])
-            faded.append(chunk)
+        for c0 in range(0, T // P, per_bank):
+            bank = psum.tile([P, 2, 2, P], F32, name="old_turned%d" % c0, tag="turn", bufs=2)
+            for k in range(per_bank):
+                for e in range(turned_blocks):
+                    col = P * (c0 + k)
+                    nc.tensor.transpose(bank[:, k, e, :], old_blocks[POOL_BLOCKS + e][:, col : col + P], ident[:])
+            for k in range(per_bank):
+                chunk = sb.tile([P, turned_blocks, P], F32, name="faded%d" % (c0 + k))
+                nc.scalar.activation(chunk[:], bank[:, k, :, :], ACT.Copy, scale=fade_col[:, c0 + k : c0 + k + 1])
+                faded.append(chunk)
 
+        for h in range(I // P):
+            for b in range(2):
+                nc.vector.tensor_copy(
+                    windows[b][:].indirect(list_i[:, P // 16 * h : P // 16 * (h + 1)]), grads[0][:, b, P * h : P * (h + 1)]
+                )
         for b in range(BLOCKS):
+            window = windows[b % WINDOWS]
+            if b >= 2:
+                nc.vector.tensor_copy(window[:].indirect(list_i[:]), grads[1][:, b - 2, :])
+            if b < POOL_BLOCKS:
+                result = sb.tile([P, T], F32, name="result%d" % b)
+                nc.gpsimd.tensor_tensor(result[:], kept[b][:], window[:], ALU.add)
+                nc.sync.dma_start(out[P * b : P * (b + 1), :], result[:])
+                continue
             for h in range(T // BANK):
                 bank = psum.tile([P, BANK], F32, name="back%d_%d" % (b, h), tag="back", bufs=3)
                 for k in range(BANK // P):
                     c = h * (BANK // P) + k
-                    nc.tensor.transpose(bank[:, P * k : P * (k + 1)], faded[c][:, P * b : P * (b + 1)], ident[:])
+                    nc.tensor.transpose(bank[:, P * k : P * (k + 1)], faded[c][:, b - POOL_BLOCKS, :], ident[:])
                 result = sb.tile([P, BANK], F32, name="result%d_%d" % (b, h))
-                nc.vector.tensor_tensor(result[:], bank[:], windows[b][:, BANK * h : BANK * (h + 1)], ALU.add)
+                nc.vector.tensor_tensor(result[:], bank[:], window[:, BANK * h : BANK * (h + 1)], ALU.add)
                 nc.sync.dma_start(out[P * b : P * (b + 1), BANK * h : BANK * (h + 1)], result[:])

@@ -44,12 +44,12 @@ def tile_attend_bpairteams_x_kernel(tc, taba, tabb_words, tabb_scales, stake, bi
         taba_rows = taba.rearrange("(p t) u -> p t u", t=PACK)
         a01 = sb.tile([P, 2, T], F32, name="a01")
         nc.sync.dma_start(a01[:], taba_rows[:, 0:2, :])
-        list_i = lists.tile([P, I // 16], U16, name="list_i")
-        nc.sync.dma_start(list_i[:], offs)
         for q in range(4):
             nc.scalar.dma_start(
                 scale_pool[32 * q : 32 * q + 4, :].bitcast(I32), tabb_scales[0, 4 * q : 4 * q + 4, :].bitcast(I32)
             )
+        list_i = lists.tile([P, I // 16], U16, name="list_i")
+        nc.sync.dma_start(list_i[:], offs)
         a_planes = [a01[:, 0, :], a01[:, 1, :]]
         for t in (2, 3):
             plane = sb.tile([P, T], F32, name="a_plane%d" % t)
@@ -96,13 +96,13 @@ def tile_attend_bpairteams_x_kernel(tc, taba, tabb_words, tabb_scales, stake, bi
 
         picked = [gather_brows(0)]
 
-        fade_turned = psum.tile([P, BANK], F32, name="fade_turned", tag="back", bufs=3)
+        fade_turned = psum.tile([P, BANK], F32, name="fade_turned", tag="back", bufs=4)
         nc.tensor.transpose(fade_turned[:, 0:P], fade_rows[:], ident[:])
         fade_col = sb.tile([P, T // P], F32, name="fade_col")
         nc.scalar.copy(fade_col[:], fade_turned[:, 0 : T // P])
         fade_all = sb.tile([P, T], F32, name="fade_all")
         for h in range(T // BANK):
-            bank = psum.tile([P, BANK], F32, name="fade_spread%d" % h, tag="back", bufs=3)
+            bank = psum.tile([P, BANK], F32, name="fade_spread%d" % h, tag="back", bufs=4)
             for k in range(BANK // P):
                 c = h * (BANK // P) + k
                 nc.tensor.transpose(bank[:, P * k : P * (k + 1)], fade_col[:, c : c + 1].to_broadcast([P, P]), ident[:])
@@ -144,12 +144,12 @@ def tile_attend_bpairteams_x_kernel(tc, taba, tabb_words, tabb_scales, stake, bi
                 )
                 scores.append(bank[:, e, :])
 
-        small = psum.tile([P, I], F32, name="small")
+        small = psum.tile([P, I], F32, name="small", tag="back", bufs=4)
         for h in range(I // P):
             nc.tensor.transpose(small[:, P * h : P * (h + 1)], stake_rows[:, h, :], ident[:])
 
         b_woven = [sb.tile([P, 2 * P, PACK], BF16, name="b_woven%d" % pair, align_bytes=64) for pair in range(2)]
-        b_codes = [sb.tile([P, 2 * P], U32, name="b_codes%d" % pair, align_bytes=64) for pair in range(2)]
+        b_codes = []
         b_scales = [sb.tile([P, 2 * P], U8, name="b_scales%d" % pair, align_bytes=64) for pair in range(2)]
 
         def turn_brows(pair, two):
@@ -163,7 +163,8 @@ def tile_attend_bpairteams_x_kernel(tc, taba, tabb_words, tabb_scales, stake, bi
                 bank[:].rearrange("p e u d -> p e d u"),
             )
 
-        def quantise_brows(pair):
+        def quantise_brows(pair, tag):
+            b_codes.append(sb.tile([P, 2 * P], U32, name="b_codes%d" % pair, tag=tag, align_bytes=64))
             nc.vector.quantize_mx(
                 out=b_codes[pair][:].bitcast(FP8X4),
                 scales=b_scales[pair][:],
@@ -185,21 +186,19 @@ def tile_attend_bpairteams_x_kernel(tc, taba, tabb_words, tabb_scales, stake, bi
         turn_brows(0, picked[0:2])
         picked.append(gather_brows(3))
         turn_brows(1, picked[2:4])
-        low = sb.tile([P, I], F32, name="low")
-        high = sb.tile([P, I], F32, name="high")
+        halves = sb.tile([P, 2, I], F32, name="halves")
         chance = sb.tile([P, I], F32, name="chance", tag="hold0", align_bytes=64)
-        nc.vector.tensor_tensor(low[:], pos[:, 0, :], pos[:, 1, :], ALU.mult)
-        nc.vector.tensor_tensor(high[:], pos[:, 2, :], pos[:, 3, :], ALU.mult)
-        nc.vector.tensor_tensor(chance[:], low[:], high[:], ALU.mult)
+        nc.vector.tensor_tensor(halves[:], pos[:, 0:2, :], pos[:, 2:4, :], ALU.mult)
+        nc.vector.tensor_tensor(chance[:], halves[:, 0, :], halves[:, 1, :], ALU.mult)
         plus_one = sb.tile([P, I], F32, name="plus_one")
         nc.vector.tensor_scalar_add(plus_one[:], chance[:], 1.0)
         staked = sb.tile([P, I], F32, name="staked")
-        nc.vector.tensor_tensor(staked[:], small[:, 0:I], chance[:], ALU.mult)
+        nc.vector.tensor_tensor(staked[:], chance[:], small[:, 0:I], ALU.mult)
         inverse = sb.tile([P, I], F32, name="inverse")
         nc.vector.reciprocal(inverse[:], plus_one[:])
-        team = sb.tile([P, I], F32, name="team")
+        team = sb.tile([P, I], F32, name="team", tag="hold2", align_bytes=64)
         nc.vector.tensor_tensor(team[:], staked[:], inverse[:], ALU.mult)
-        quantise_brows(0)
+        quantise_brows(0, "b_codes")
         g_codes = sb.tile([P, I], U32, name="g_codes", align_bytes=64)
         g_scales = sb.tile([P, I], U8, name="g_scales", align_bytes=64)
         grads = [sb.tile([P, 2, I], F32, name="grads%d" % pair) for pair in range(2)]
@@ -226,8 +225,8 @@ def tile_attend_bpairteams_x_kernel(tc, taba, tabb_words, tabb_scales, stake, bi
                 team[:, cols].rearrange("p (c i) -> p c i", i=4).unsqueeze(2).to_broadcast([P, P // 4, PACK, 4]),
                 ALU.mult,
             )
-            if h == 0:
-                quantise_brows(1)
+            if h == 1:
+                quantise_brows(1, "hold2")
             nc.vector.quantize_mx(
                 out=g_codes[:, cols].bitcast(FP8X4), scales=g_scales[:, cols], in_=g_woven[:].rearrange("p i r -> p (i r)")
             )
@@ -264,18 +263,18 @@ def tile_attend_bpairteams_x_kernel(tc, taba, tabb_words, tabb_scales, stake, bi
                 )
         for b in range(BLOCKS):
             window = windows[b % WINDOWS]
-            if b >= 2:
-                nc.vector.tensor_copy(window[:].indirect(list_i[:]), grads[1][:, b - 2, :])
             if b < POOL_BLOCKS:
                 result = sb.tile([P, T], F32, name="result%d" % b)
                 nc.gpsimd.tensor_tensor(result[:], kept[b][:], window[:], ALU.add)
                 nc.sync.dma_start(out[P * b : P * (b + 1), :], result[:])
                 continue
+            nc.vector.tensor_copy(window[:].indirect(list_i[:]), grads[1][:, b - 2, :])
             for h in range(T // BANK):
-                bank = psum.tile([P, BANK], F32, name="back%d_%d" % (b, h), tag="back", bufs=3)
+                cols = slice(BANK * h, BANK * (h + 1))
+                bank = psum.tile([P, BANK], F32, name="back%d_%d" % (b, h), tag="back", bufs=4)
                 for k in range(BANK // P):
                     c = h * (BANK // P) + k
                     nc.tensor.transpose(bank[:, P * k : P * (k + 1)], faded[c][:, b - POOL_BLOCKS, :], ident[:])
                 result = sb.tile([P, BANK], F32, name="result%d_%d" % (b, h))
-                nc.vector.tensor_tensor(result[:], bank[:], window[:, BANK * h : BANK * (h + 1)], ALU.add)
-                nc.sync.dma_start(out[P * b : P * (b + 1), BANK * h : BANK * (h + 1)], result[:])
+                nc.vector.tensor_tensor(result[:], window[:, cols], bank[:], ALU.add)
+                nc.sync.dma_start(out[P * b : P * (b + 1), cols], result[:])

@@ -19,11 +19,13 @@ ALU = mybir.AluOpType
 
 P = 128
 PACK = 4
+RUN = 4
 BANK = 512
+LIST_ROWS = 16
 BLOCKS = D // P
 VECTOR_BLOCKS = (1, 2)
+GPSIMD_BLOCKS = 2
 WINDOWS = 3
-POOL_BLOCKS = 2
 
 
 def tile_attend_bpairteams_x_kernel(tc, taba, tabb_words, tabb_scales, stake, bias, js, brows, old, fade, offs, offs2, out):
@@ -35,22 +37,22 @@ def tile_attend_bpairteams_x_kernel(tc, taba, tabb_words, tabb_scales, stake, bi
 
         scale_pool = sb.tile([P, U], U8, name="scale_pool")
         nc.vector.memset(scale_pool[:].bitcast(I32), 0)
-        list_j = lists.tile([P, J // 16], U16, name="list_j")
+        list_j = lists.tile([P, J // LIST_ROWS], U16, name="list_j")
         nc.sync.dma_start(list_j[:], offs2)
         word_pool = sb.tile([P, U], U16, name="word_pool")
         nc.sync.dma_start(word_pool[:].bitcast(I32), tabb_words[0].bitcast(I32))
         b_blocks = [sb.tile([P, U], F32, name="b_block%d" % b) for b in range(BLOCKS)]
         nc.sync.dma_start(b_blocks[0][:], brows[0:P, :])
         taba_rows = taba.rearrange("(p t) u -> p t u", t=PACK)
-        a01 = sb.tile([P, 2, T], F32, name="a01")
-        nc.sync.dma_start(a01[:], taba_rows[:, 0:2, :])
+        a_first = sb.tile([P, 2, T], F32, name="a_first")
+        nc.sync.dma_start(a_first[:], taba_rows[:, 0:2, :])
         for q in range(4):
             nc.scalar.dma_start(
                 scale_pool[32 * q : 32 * q + 4, :].bitcast(I32), tabb_scales[0, 4 * q : 4 * q + 4, :].bitcast(I32)
             )
-        list_i = lists.tile([P, I // 16], U16, name="list_i")
+        list_i = lists.tile([P, I // LIST_ROWS], U16, name="list_i")
         nc.sync.dma_start(list_i[:], offs)
-        a_planes = [a01[:, 0, :], a01[:, 1, :]]
+        a_planes = [a_first[:, 0, :], a_first[:, 1, :]]
         for t in (2, 3):
             plane = sb.tile([P, T], F32, name="a_plane%d" % t)
             nc.sync.dma_start(plane[:], taba_rows[:, t, :])
@@ -60,27 +62,24 @@ def tile_attend_bpairteams_x_kernel(tc, taba, tabb_words, tabb_scales, stake, bi
         js_col = sb.tile([P, PACK], F32, name="js_col")
         nc.scalar.dma_start(js_col[:], js[0].rearrange("(p r) -> p r", r=PACK))
         stake_rows = sb.tile([P, I // P, G], F32, name="stake_rows")
+        old_blocks = [sb.tile([P, T], F32, name="old_block%d" % b) for b in range(BLOCKS)]
+        nc.sync.dma_start(b_blocks[1][:], brows[P : 2 * P, :])
+        nc.sync.dma_start(stake_rows[:], stake.rearrange("(h p) g -> p h g", p=P))
+        nc.sync.dma_start(b_blocks[2][:], brows[2 * P : 3 * P, :])
+        nc.sync.dma_start(old_blocks[0][:], old[0:P, :])
+        nc.sync.dma_start(b_blocks[3][:], brows[3 * P : 4 * P, :])
         for b in range(1, BLOCKS):
-            nc.sync.dma_start(b_blocks[b][:], brows[P * b : P * (b + 1), :])
-            if b == 1:
-                nc.sync.dma_start(stake_rows[:], stake.rearrange("(h p) g -> p h g", p=P))
+            nc.sync.dma_start(old_blocks[b][:], old[P * b : P * (b + 1), :])
         fade_rows = sb.tile([P, P], F32, name="fade_rows")
         nc.gpsimd.memset(fade_rows[:], 0.0)
         nc.gpsimd.dma_start(fade_rows[0 : T // P, :], fade[0].rearrange("(c p) -> c p", p=P))
-        old_blocks = []
-        for b in range(BLOCKS):
-            block = sb.tile([P, T], F32, name="old_block%d" % b)
-            nc.sync.dma_start(block[:], old[P * b : P * (b + 1), :])
-            old_blocks.append(block)
 
         ident = sb.tile([P, P], F32, name="ident")
         make_identity(nc, ident[:])
-        warm = sb.tile([P, 1], F32, name="warm")
-        nc.scalar.activation(warm[:], ident[:, 0:1], ACT.Sigmoid)
 
         windows = []
-        for b in range(WINDOWS):
-            window = sb.tile([P, T], F32, name="window%d" % b)
+        for w in range(WINDOWS):
+            window = sb.tile([P, T], F32, name="window%d" % w)
             nc.vector.memset(window[:], 0.0)
             windows.append(window)
 
@@ -129,35 +128,33 @@ def tile_attend_bpairteams_x_kernel(tc, taba, tabb_words, tabb_scales, stake, bi
         nc.gpsimd.tensor_scalar(neg_bias[:], bias_col[:], -1.0, 0.0, ALU.mult, ALU.add)
 
         scores = []
-        for pair in range(2):
-            bank = psum.tile([P, 2, I], F32, name="scores%d" % pair, tag="mx", bufs=2)
-            for e in range(2):
-                r = 2 * pair + e
-                nc.tensor.matmul_mx(
-                    out=bank[:, e, :],
-                    lhsT=words_dealt[:, r, :].bitcast(FP4X4),
-                    lhsT_scale=scales_dealt[:, r, :],
-                    rhs=a_codes[:].bitcast(FP8X4),
-                    rhs_scale=a_scales[:],
-                    start=True,
-                    stop=True,
-                )
-                scores.append(bank[:, e, :])
+        for r in range(PACK):
+            bank = psum.tile([P, I], F32, name="scores%d" % r, tag=("mx", "turn")[r // 2], bufs=2)
+            nc.tensor.matmul_mx(
+                out=bank[:],
+                lhsT=words_dealt[:, r, :].bitcast(FP4X4),
+                lhsT_scale=scales_dealt[:, r, :],
+                rhs=a_codes[:].bitcast(FP8X4),
+                rhs_scale=a_scales[:],
+                start=True,
+                stop=True,
+            )
+            scores.append(bank[:])
 
-        small = psum.tile([P, I], F32, name="small", tag="back", bufs=4)
+        stake_turned = psum.tile([P, I], F32, name="stake_turned", tag="back", bufs=4)
         for h in range(I // P):
-            nc.tensor.transpose(small[:, P * h : P * (h + 1)], stake_rows[:, h, :], ident[:])
+            nc.tensor.transpose(stake_turned[:, P * h : P * (h + 1)], stake_rows[:, h, :], ident[:])
 
         b_woven = [sb.tile([P, 2 * P, PACK], BF16, name="b_woven%d" % pair, align_bytes=64) for pair in range(2)]
         b_codes = []
         b_scales = [sb.tile([P, 2 * P], U8, name="b_scales%d" % pair, align_bytes=64) for pair in range(2)]
 
-        def turn_brows(pair, two):
+        def turn_brows(pair, two_blocks):
             bank = psum.tile([P, 2, 2, P], F32, name="b_turned%d" % pair, tag="turn", bufs=2)
             for e in range(2):
-                pairs = two[e][:].bitcast(F32)
+                j_pairs = two_blocks[e][:].bitcast(F32)
                 for u in range(2):
-                    nc.tensor.transpose(bank[:, e, u, :], pairs[:, u : J // 2 : 2], ident[:])
+                    nc.tensor.transpose(bank[:, e, u, :], j_pairs[:, u : J // 2 : 2], ident[:])
             nc.scalar.copy(
                 b_woven[pair][:].rearrange("p d t -> p (d t)").bitcast(F32).rearrange("p (e d u) -> p e d u", e=2, u=2),
                 bank[:].rearrange("p e u d -> p e d u"),
@@ -186,19 +183,20 @@ def tile_attend_bpairteams_x_kernel(tc, taba, tabb_words, tabb_scales, stake, bi
         turn_brows(0, picked[0:2])
         picked.append(gather_brows(3))
         turn_brows(1, picked[2:4])
-        halves = sb.tile([P, 2, I], F32, name="halves")
-        chance = sb.tile([P, I], F32, name="chance", tag="hold0", align_bytes=64)
-        nc.vector.tensor_tensor(halves[:], pos[:, 0:2, :], pos[:, 2:4, :], ALU.mult)
-        nc.vector.tensor_tensor(chance[:], halves[:, 0, :], halves[:, 1, :], ALU.mult)
+        two_products = sb.tile([P, 2, I], F32, name="two_products", tag="hold0", align_bytes=64)
+        chance = sb.tile([P, I], F32, name="chance")
+        nc.vector.tensor_tensor(two_products[:], pos[:, 0:2, :], pos[:, 2:4, :], ALU.mult)
+        nc.vector.tensor_tensor(chance[:], two_products[:, 0, :], two_products[:, 1, :], ALU.mult)
         plus_one = sb.tile([P, I], F32, name="plus_one")
         nc.vector.tensor_scalar_add(plus_one[:], chance[:], 1.0)
         staked = sb.tile([P, I], F32, name="staked")
-        nc.vector.tensor_tensor(staked[:], chance[:], small[:, 0:I], ALU.mult)
+        nc.vector.tensor_tensor(staked[:], chance[:], stake_turned[:], ALU.mult)
         inverse = sb.tile([P, I], F32, name="inverse")
         nc.vector.reciprocal(inverse[:], plus_one[:])
         team = sb.tile([P, I], F32, name="team", tag="hold2", align_bytes=64)
         nc.vector.tensor_tensor(team[:], staked[:], inverse[:], ALU.mult)
         quantise_brows(0, "b_codes")
+
         g_codes = sb.tile([P, I], U32, name="g_codes", align_bytes=64)
         g_scales = sb.tile([P, I], U8, name="g_scales", align_bytes=64)
         grads = [sb.tile([P, 2, I], F32, name="grads%d" % pair) for pair in range(2)]
@@ -220,12 +218,12 @@ def tile_attend_bpairteams_x_kernel(tc, taba, tabb_words, tabb_scales, stake, bi
             cols = slice(P * h, P * (h + 1))
             g_woven = sb.tile([P, P, PACK], BF16, name="g_woven%d" % h, tag="hold1", align_bytes=64)
             nc.vector.tensor_tensor(
-                g_woven[:].rearrange("p (c i) r -> p c r i", i=4),
-                neg_js[:, :, cols].rearrange("p r (c i) -> p c r i", i=4),
-                team[:, cols].rearrange("p (c i) -> p c i", i=4).unsqueeze(2).to_broadcast([P, P // 4, PACK, 4]),
+                g_woven[:].rearrange("p (c i) r -> p c r i", i=RUN),
+                neg_js[:, :, cols].rearrange("p r (c i) -> p c r i", i=RUN),
+                team[:, cols].rearrange("p (c i) -> p c i", i=RUN).unsqueeze(2).to_broadcast([P, P // RUN, PACK, RUN]),
                 ALU.mult,
             )
-            if h == 1:
+            if h == I // P - 1:
                 quantise_brows(1, "hold2")
             nc.vector.quantize_mx(
                 out=g_codes[:, cols].bitcast(FP8X4), scales=g_scales[:, cols], in_=g_woven[:].rearrange("p i r -> p (i r)")
@@ -237,36 +235,38 @@ def tile_attend_bpairteams_x_kernel(tc, taba, tabb_words, tabb_scales, stake, bi
         nc.scalar.copy(grads[1][:], second_bank[:])
 
         kept = []
-        for b in range(POOL_BLOCKS):
+        for b in range(GPSIMD_BLOCKS):
             product = sb.tile([P, T], F32, name="kept%d" % b, tag="hold%d" % b, align_bytes=64)
             nc.gpsimd.tensor_tensor(product[:], old_blocks[b][:], fade_all[:], ALU.mult)
             kept.append(product)
 
-        turned_blocks = BLOCKS - POOL_BLOCKS
+        turned_blocks = BLOCKS - GPSIMD_BLOCKS
         per_bank = BANK // (P * turned_blocks)
         faded = []
         for c0 in range(0, T // P, per_bank):
-            bank = psum.tile([P, 2, 2, P], F32, name="old_turned%d" % c0, tag="turn", bufs=2)
+            bank = psum.tile([P, per_bank, turned_blocks, P], F32, name="old_turned%d" % c0, tag="turn", bufs=2)
             for k in range(per_bank):
                 for e in range(turned_blocks):
                     col = P * (c0 + k)
-                    nc.tensor.transpose(bank[:, k, e, :], old_blocks[POOL_BLOCKS + e][:, col : col + P], ident[:])
+                    nc.tensor.transpose(bank[:, k, e, :], old_blocks[GPSIMD_BLOCKS + e][:, col : col + P], ident[:])
             for k in range(per_bank):
                 chunk = sb.tile([P, turned_blocks, P], F32, name="faded%d" % (c0 + k))
                 nc.scalar.activation(chunk[:], bank[:, k, :, :], ACT.Copy, scale=fade_col[:, c0 + k : c0 + k + 1])
                 faded.append(chunk)
 
         for h in range(I // P):
+            entries = list_i[:, P // LIST_ROWS * h : P // LIST_ROWS * (h + 1)]
             for b in range(2):
-                nc.vector.tensor_copy(
-                    windows[b][:].indirect(list_i[:, P // 16 * h : P // 16 * (h + 1)]), grads[0][:, b, P * h : P * (h + 1)]
-                )
+                nc.vector.tensor_copy(windows[b][:].indirect(entries), grads[0][:, b, P * h : P * (h + 1)])
         for b in range(BLOCKS):
             window = windows[b % WINDOWS]
-            if b < POOL_BLOCKS:
-                result = sb.tile([P, T], F32, name="result%d" % b)
-                nc.gpsimd.tensor_tensor(result[:], kept[b][:], window[:], ALU.add)
-                nc.sync.dma_start(out[P * b : P * (b + 1), :], result[:])
+            if b < GPSIMD_BLOCKS:
+                width = T // (b + 1)
+                for start in range(0, T, width):
+                    cols = slice(start, start + width)
+                    result = sb.tile([P, width], F32, name="result%d_%d" % (b, start))
+                    nc.gpsimd.tensor_tensor(result[:], kept[b][:, cols], window[:, cols], ALU.add)
+                    nc.sync.dma_start(out[P * b : P * (b + 1), cols], result[:])
                 continue
             nc.vector.tensor_copy(window[:].indirect(list_i[:]), grads[1][:, b - 2, :])
             for h in range(T // BANK):
@@ -274,7 +274,7 @@ def tile_attend_bpairteams_x_kernel(tc, taba, tabb_words, tabb_scales, stake, bi
                 bank = psum.tile([P, BANK], F32, name="back%d_%d" % (b, h), tag="back", bufs=4)
                 for k in range(BANK // P):
                     c = h * (BANK // P) + k
-                    nc.tensor.transpose(bank[:, P * k : P * (k + 1)], faded[c][:, b - POOL_BLOCKS, :], ident[:])
+                    nc.tensor.transpose(bank[:, P * k : P * (k + 1)], faded[c][:, b - GPSIMD_BLOCKS, :], ident[:])
                 result = sb.tile([P, BANK], F32, name="result%d_%d" % (b, h))
                 nc.vector.tensor_tensor(result[:], window[:, cols], bank[:], ALU.add)
                 nc.sync.dma_start(out[P * b : P * (b + 1), cols], result[:])

from contextlib import ExitStack

import concourse.mybir as mybir
from concourse.masks import make_identity

D, T, U, I, J, G = 512, 1024, 1024, 256, 512, 128
FLOPS = 2 * D * I * J + 2 * J * D * I

F32 = mybir.dt.float32
BF16 = mybir.dt.bfloat16
I32 = mybir.dt.int32
U32 = mybir.dt.uint32
U16 = mybir.dt.uint16
U8 = mybir.dt.uint8
FP8X4 = mybir.dt.float8_e4m3fn_x4
FP4X4 = mybir.dt.float4_e2m1fn_x4
ACT = mybir.ActivationFunctionType
ALU = mybir.AluOpType

P = 128
PACK = 4
RUN = 4
BANK = 512
LIST_ROWS = 16
BLOCKS = D // P
VECTOR_BLOCKS = (1, 2)
GPSIMD_BLOCKS = 2
WINDOWS = 3


def tile_attend_bpairteams_x_kernel(tc, taba, tabb_words, tabb_scales, stake, bias, js, brows, old, fade, offs, offs2, out):
    nc = tc.nc
    with ExitStack() as ctx:
        lists = ctx.enter_context(tc.tile_pool(name="lists", bufs=1))
        sb = ctx.enter_context(tc.tile_pool(name="sb", bufs=1))
        psum = ctx.enter_context(tc.psum_pool(name="psum", bufs=1))

        scale_pool = sb.tile([P, U], U8, name="scale_pool")
        nc.vector.memset(scale_pool[:].bitcast(I32), 0)
        list_j = lists.tile([P, J // LIST_ROWS], U16, name="list_j")
        nc.sync.dma_start(list_j[:], offs2)
        word_pool = sb.tile([P, U], U16, name="word_pool")
        nc.sync.dma_start(word_pool[:].bitcast(I32), tabb_words[0].bitcast(I32))
        b_blocks = [sb.tile([P, U], F32, name="b_block%d" % b) for b in range(BLOCKS)]
        nc.sync.dma_start(b_blocks[0][:], brows[0:P, :])
        taba_rows = taba.rearrange("(p t) u -> p t u", t=PACK)
        a_first = sb.tile([P, 2, T], F32, name="a_first")
        nc.sync.dma_start(a_first[:], taba_rows[:, 0:2, :])
        for q in range(4):
            nc.scalar.dma_start(
                scale_pool[32 * q : 32 * q + 4, :].bitcast(I32), tabb_scales[0, 4 * q : 4 * q + 4, :].bitcast(I32)
            )
        list_i = lists.tile([P, I // LIST_ROWS], U16, name="list_i")
        nc.sync.dma_start(list_i[:], offs)
        a_planes = [a_first[:, 0, :], a_first[:, 1, :]]
        for t in (2, 3):
            plane = sb.tile([P, T], F32, name="a_plane%d" % t)
            nc.sync.dma_start(plane[:], taba_rows[:, t, :])
            a_planes.append(plane[:])
        bias_col = sb.tile([P, PACK], F32, name="bias_col")
        nc.scalar.dma_start(bias_col[:], bias[0].rearrange("(p r) -> p r", r=PACK))
        js_col = sb.tile([P, PACK], F32, name="js_col")
        nc.scalar.dma_start(js_col[:], js[0].rearrange("(p r) -> p r", r=PACK))
        stake_rows = sb.tile([P, I // P, G], F32, name="stake_rows")
        old_blocks = [sb.tile([P, T], F32, name="old_block%d" % b) for b in range(BLOCKS)]
        nc.sync.dma_start(b_blocks[1][:], brows[P : 2 * P, :])
        nc.sync.dma_start(stake_rows[:], stake.rearrange("(h p) g -> p h g", p=P))
        nc.sync.dma_start(b_blocks[2][:], brows[2 * P : 3 * P, :])
        nc.sync.dma_start(old_blocks[0][:], old[0:P, :])
        nc.sync.dma_start(b_blocks[3][:], brows[3 * P : 4 * P, :])
        for b in range(1, BLOCKS):
            nc.sync.dma_start(old_blocks[b][:], old[P * b : P * (b + 1), :])
        fade_rows = sb.tile([P, P], F32, name="fade_rows")
        nc.gpsimd.memset(fade_rows[:], 0.0)
        nc.gpsimd.dma_start(fade_rows[0 : T // P, :], fade[0].rearrange("(c p) -> c p", p=P))

        ident = sb.tile([P, P], F32, name="ident")
        make_identity(nc, ident[:])

        windows = []
        for w in range(WINDOWS):
            window = sb.tile([P, T], F32, name="window%d" % w)
            nc.vector.memset(window[:], 0.0)
            windows.append(window)

        def gather_brows(b):
            columns = sb.tile([P, J], BF16, name="b_picked%d" % b)
            if b in VECTOR_BLOCKS:
                nc.vector.tensor_copy(columns[:], b_blocks[b][:].indirect(list_j[:]))
            else:
                narrow = sb.tile([P, U], BF16, name="b_narrow%d" % b)
                nc.scalar.activation(narrow[:], b_blocks[b][:], ACT.Copy)
                nc.scalar.activation(columns[:], narrow[:].indirect(list_j[:]), ACT.Copy)
            return columns

        picked = [gather_brows(0)]

        fade_turned = psum.tile([P, BANK], F32, name="fade_turned", tag="back", bufs=4)
        nc.tensor.transpose(fade_turned[:, 0:P], fade_rows[:], ident[:])
        fade_col = sb.tile([P, T // P], F32, name="fade_col")
        nc.scalar.copy(fade_col[:], fade_turned[:, 0 : T // P])
        fade_all = sb.tile([P, T], F32, name="fade_all")
        for h in range(T // BANK):
            bank = psum.tile([P, BANK], F32, name="fade_spread%d" % h, tag="back", bufs=4)
            for k in range(BANK // P):
                c = h * (BANK // P) + k
                nc.tensor.transpose(bank[:, P * k : P * (k + 1)], fade_col[:, c : c + 1].to_broadcast([P, P]), ident[:])
            nc.scalar.copy(fade_all[:, BANK * h : BANK * (h + 1)], bank[:])

        words_j = sb.tile([P, J], U16, name="words_j")
        nc.vector.tensor_copy(words_j[:], word_pool[:].indirect(list_j[:]))
        words_dealt = sb.tile([P, PACK, G], U16, name="words_dealt", align_bytes=64)
        nc.vector.tensor_copy(words_dealt[:], words_j[:].rearrange("p (g r) -> p r g", r=PACK))
        scales_j = sb.tile([P, J], U8, name="scales_j")
        nc.vector.tensor_copy(scales_j[:], scale_pool[:].indirect(list_j[:]))
        scales_dealt = sb.tile([P, PACK, G], U8, name="scales_dealt", align_bytes=64)
        nc.vector.tensor_copy(scales_dealt[:], scales_j[:].rearrange("p (g r) -> p r g", r=PACK))

        a_woven = sb.tile([P, I, PACK], BF16, name="a_woven", align_bytes=64)
        for t in range(PACK):
            nc.vector.tensor_copy(a_woven[:, :, t], a_planes[t].indirect(list_i[:]))
        a_codes = sb.tile([P, I], U32, name="a_codes", align_bytes=64)
        a_scales = sb.tile([P, I], U8, name="a_scales", align_bytes=64)
        nc.vector.quantize_mx(
            out=a_codes[:].bitcast(FP8X4), scales=a_scales[:], in_=a_woven[:].rearrange("p i t -> p (i t)")
        )
        neg_bias = sb.tile([P, PACK], F32, name="neg_bias")
        nc.gpsimd.tensor_scalar(neg_bias[:], bias_col[:], -1.0, 0.0, ALU.mult, ALU.add)

        scores = []
        for r in range(PACK):
            bank = psum.tile([P, I], F32, name="scores%d" % r, tag=("mx", "turn")[r // 2], bufs=2)
            nc.tensor.matmul_mx(
                out=bank[:],
                lhsT=words_dealt[:, r, :].bitcast(FP4X4),
                lhsT_scale=scales_dealt[:, r, :],
                rhs=a_codes[:].bitcast(FP8X4),
                rhs_scale=a_scales[:],
                start=True,
                stop=True,
            )
            scores.append(bank[:])

        stake_turned = psum.tile([P, I], F32, name="stake_turned", tag="back", bufs=4)
        for h in range(I // P):
            nc.tensor.transpose(stake_turned[:, P * h : P * (h + 1)], stake_rows[:, h, :], ident[:])

        b_woven = [sb.tile([P, 2 * P, PACK], BF16, name="b_woven%d" % pair, align_bytes=64) for pair in range(2)]
        b_codes = []
        b_scales = [sb.tile([P, 2 * P], U8, name="b_scales%d" % pair, align_bytes=64) for pair in range(2)]

        def turn_brows(pair, two_blocks):
            bank = psum.tile([P, 2, 2, P], F32, name="b_turned%d" % pair, tag="turn", bufs=2)
            for e in range(2):
                j_pairs = two_blocks[e][:].bitcast(F32)
                for u in range(2):
                    nc.tensor.transpose(bank[:, e, u, :], j_pairs[:, u : J // 2 : 2], ident[:])
            nc.scalar.copy(
                b_woven[pair][:].rearrange("p d t -> p (d t)").bitcast(F32).rearrange("p (e d u) -> p e d u", e=2, u=2),
                bank[:].rearrange("p e u d -> p e d u"),
            )

        def quantise_brows(pair, tag):
            b_codes.append(sb.tile([P, 2 * P], U32, name="b_codes%d" % pair, tag=tag, align_bytes=64))
            nc.vector.quantize_mx(
                out=b_codes[pair][:].bitcast(FP8X4),
                scales=b_scales[pair][:],
                in_=b_woven[pair][:].rearrange("p d t -> p (d t)"),
            )

        picked.append(gather_brows(1))
        picked.append(gather_brows(2))

        pos = sb.tile([P, PACK, I], F32, name="pos")
        neg = sb.tile([P, PACK, I], F32, name="neg")
        neg_js = sb.tile([P, PACK, I], F32, name="neg_js")
        for r in range(PACK):
            nc.scalar.activation(pos[:, r, :], scores[r], ACT.Sigmoid, bias=bias_col[:, r : r + 1])
        for r in range(PACK):
            nc.scalar.activation(neg[:, r, :], scores[r], ACT.Sigmoid, bias=neg_bias[:, r : r + 1], scale=-1.0)
        for r in range(PACK):
            nc.scalar.activation(neg_js[:, r, :], neg[:, r, :], ACT.Copy, scale=js_col[:, r : r + 1])
        turn_brows(0, picked[0:2])
        picked.append(gather_brows(3))
        turn_brows(1, picked[2:4])
        two_products = sb.tile([P, 2, I], F32, name="two_products", tag="hold0", align_bytes=64)
        chance = sb.tile([P, I], F32, name="chance")
        nc.vector.tensor_tensor(two_products[:], pos[:, 0:2, :], pos[:, 2:4, :], ALU.mult)
        nc.vector.tensor_tensor(chance[:], two_products[:, 0, :], two_products[:, 1, :], ALU.mult)
        plus_one = sb.tile([P, I], F32, name="plus_one")
        nc.vector.tensor_scalar_add(plus_one[:], chance[:], 1.0)
        staked = sb.tile([P, I], F32, name="staked")
        nc.vector.tensor_tensor(staked[:], chance[:], stake_turned[:], ALU.mult)
        inverse = sb.tile([P, I], F32, name="inverse")
        nc.vector.reciprocal(inverse[:], plus_one[:])
        team = sb.tile([P, I], F32, name="team", tag="hold2", align_bytes=64)
        nc.vector.tensor_tensor(team[:], staked[:], inverse[:], ALU.mult)
        quantise_brows(0, "b_codes")

        g_codes = sb.tile([P, I], U32, name="g_codes", align_bytes=64)
        g_scales = sb.tile([P, I], U8, name="g_scales", align_bytes=64)
        grads = [sb.tile([P, 2, I], F32, name="grads%d" % pair) for pair in range(2)]

        def second_product(pair, bank, cols):
            for e in range(2):
                nc.tensor.matmul_mx(
                    out=bank[:, e, :],
                    lhsT=b_codes[pair][:, P * e : P * (e + 1)].bitcast(FP8X4),
                    lhsT_scale=b_scales[pair][:, P * e : P * (e + 1)],
                    rhs=g_codes[:, cols].bitcast(FP8X4),
                    rhs_scale=g_scales[:, cols],
                    start=True,
                    stop=True,
                )

        first_bank = psum.tile([P, 2, 2, P], F32, name="grad_first", tag="mx", bufs=2)
        for h in range(I // P):
            cols = slice(P * h, P * (h + 1))
            g_woven = sb.tile([P, P, PACK], BF16, name="g_woven%d" % h, tag="hold1", align_bytes=64)
            nc.vector.tensor_tensor(
                g_woven[:].rearrange("p (c i) r -> p c r i", i=RUN),
                neg_js[:, :, cols].rearrange("p r (c i) -> p c r i", i=RUN),
                team[:, cols].rearrange("p (c i) -> p c i", i=RUN).unsqueeze(2).to_broadcast([P, P // RUN, PACK, RUN]),
                ALU.mult,
            )
            if h == I // P - 1:
                quantise_brows(1, "hold2")
            nc.vector.quantize_mx(
                out=g_codes[:, cols].bitcast(FP8X4), scales=g_scales[:, cols], in_=g_woven[:].rearrange("p i r -> p (i r)")
            )
            second_product(0, first_bank[:, h, :, :], cols)
            nc.scalar.copy(grads[0][:, :, cols], first_bank[:, h, :, :])
        second_bank = psum.tile([P, 2, I], F32, name="grad_second", tag="mx", bufs=2)
        second_product(1, second_bank[:], slice(0, I))
        nc.scalar.copy(grads[1][:], second_bank[:])

        kept = []
        for b in range(GPSIMD_BLOCKS):
            product = sb.tile([P, T], F32, name="kept%d" % b, tag="hold%d" % b, align_bytes=64)
            nc.gpsimd.tensor_tensor(product[:], old_blocks[b][:], fade_all[:], ALU.mult)
            kept.append(product)

        turned_blocks = BLOCKS - GPSIMD_BLOCKS
        per_bank = BANK // (P * turned_blocks)
        faded = []
        for c0 in range(0, T // P, per_bank):
            bank = psum.tile([P, per_bank, turned_blocks, P], F32, name="old_turned%d" % c0, tag="turn", bufs=2)
            for k in range(per_bank):
                for e in range(turned_blocks):
                    col = P * (c0 + k)
                    nc.tensor.transpose(bank[:, k, e, :], old_blocks[GPSIMD_BLOCKS + e][:, col : col + P], ident[:])
            for k in range(per_bank):
                chunk = sb.tile([P, turned_blocks, P], F32, name="faded%d" % (c0 + k))
                nc.scalar.activation(chunk[:], bank[:, k, :, :], ACT.Copy, scale=fade_col[:, c0 + k : c0 + k + 1])
                faded.append(chunk)

        for h in range(I // P):
            entries = list_i[:, P // LIST_ROWS * h : P // LIST_ROWS * (h + 1)]
            for b in range(2):
                nc.vector.tensor_copy(windows[b][:].indirect(entries), grads[0][:, b, P * h : P * (h + 1)])
        for b in range(BLOCKS):
            window = windows[b % WINDOWS]
            if b < GPSIMD_BLOCKS:
                width = T // (b + 1)
                for start in range(0, T, width):
                    cols = slice(start, start + width)
                    result = sb.tile([P, width], F32, name="result%d_%d" % (b, start))
                    nc.gpsimd.tensor_tensor(result[:], kept[b][:, cols], window[:, cols], ALU.add)
                    nc.sync.dma_start(out[P * b : P * (b + 1), cols], result[:])
                continue
            nc.vector.tensor_copy(window[:].indirect(list_i[:]), grads[1][:, b - 2, :])
            for h in range(T // BANK):
                cols = slice(BANK * h, BANK * (h + 1))
                bank = psum.tile([P, BANK], F32, name="back%d_%d" % (b, h), tag="back", bufs=4)
                for k in range(BANK // P):
                    c = h * (BANK // P) + k
                    nc.tensor.transpose(bank[:, P * k : P * (k + 1)], faded[c][:, b - GPSIMD_BLOCKS, :], ident[:])
                result = sb.tile([P, BANK], F32, name="result%d_%d" % (b, h))
                nc.vector.tensor_tensor(result[:], window[:, cols], bank[:], ALU.add)
                nc.sync.dma_start(out[P * b : P * (b + 1), cols], result[:])
